import numpy as np
import ml_dtypes


def mxq(x, axis, fmt="e4m3"):
    dtype, down = {"e4m3": (ml_dtypes.float8_e4m3fn, 7), "e5m2": (ml_dtypes.float8_e5m2, 14)}[fmt]
    v = np.moveaxis(np.asarray(x, np.float32).astype(ml_dtypes.bfloat16).astype(np.float64), axis, -1)
    blocks = v.reshape(v.shape[:-1] + (-1, 32))
    amax = np.abs(blocks).max(-1, keepdims=True)
    byte = np.maximum(np.where(amax > 0, np.frexp(amax)[1] - 1 + 127, 0) - down, 1)
    scale = np.exp2(byte - 127.0)
    codes = (blocks / scale).astype(np.float32).astype(dtype).astype(np.float64)
    return np.moveaxis((codes * scale).reshape(v.shape), -1, axis)


WIDE = False


def mx_kscale(k):
    if not WIDE:
        return np.ones(k)
    levels = np.array([10, -10, 5, -5, 0])
    if k % 512:
        return np.exp2(np.random.permutation(np.resize(levels, k // 32))).repeat(32)
    a = np.empty((k // 512, 16))
    for p in range(k // 512):
        a[p, :8] = np.random.permutation(np.resize(levels, 8))
        for g in range(8):
            far = levels[np.abs(levels - a[p, g]) >= 10]
            a[p, g + 8] = far[np.random.randint(len(far))]
    return np.exp2(a.ravel()).repeat(32)


def f64(x):
    return np.asarray(x).astype(np.float64)


E2M1 = np.array([0.0, 0.5, 1.0, 1.5, 2.0, 3.0, 4.0, 6.0, -0.0, -0.5, -1.0, -1.5, -2.0, -3.0, -4.0, -6.0])


def pack_weight(w, fmt):
    k, n = w.shape
    w = f64(np.asarray(w, np.float32).astype(ml_dtypes.bfloat16)).reshape(k // 32, 32, n)
    amax = np.abs(w).max(1)
    if fmt == "e4m3":
        byte = np.frexp(amax)[1] - 1 + 127 - 7
    else:
        mant, ex = np.frexp(amax / 6.0)
        byte = np.where(mant > 0.5, ex, ex - 1) + 127
    byte = np.clip(np.where(amax > 0, byte, 1), 1, 254)
    scaled = (w * np.exp2(127.0 - byte)[:, None, :]).reshape(k, n).astype(np.float32)
    by_word = np.ascontiguousarray(scaled.reshape(k // 512, 128, 4, n).transpose(0, 1, 3, 2))
    if fmt == "e4m3":
        words = by_word.astype(ml_dtypes.float8_e4m3fn).view(np.uint8)
    else:
        c = by_word.astype(ml_dtypes.float4_e2m1fn).view(np.uint8) & 0xF
        words = (c[..., 0::2] | (c[..., 1::2] << 4)).reshape(k // 512, 128, 2 * n)
    return np.ascontiguousarray(words), np.ascontiguousarray(byte.astype(np.uint8).reshape(k // 512, 16, n))


def unpack_weight(words, scales, fmt):
    g, _, n = scales.shape
    words = np.ascontiguousarray(words).reshape(g, 128, n, -1)
    if fmt == "e4m3":
        vals = words.view(ml_dtypes.float8_e4m3fn).astype(np.float64)
    else:
        nib = np.empty((g, 128, n, 4), np.uint8)
        nib[..., 0::2] = words & 0xF
        nib[..., 1::2] = words >> 4
        vals = E2M1[nib]
    vals = vals * np.repeat(np.exp2(scales.astype(np.float64) - 127.0), 8, axis=1)[..., None]
    return vals.transpose(0, 1, 3, 2).reshape(g * 512, n)


K, M, T = 1024, 1536, 1024


def setup_inputs():
    n = np.random.standard_normal
    s = mx_kscale(K)[:, None]
    u = mx_kscale(T)[:, None]
    q = n((K, T)) * s
    p_vc = pack_weight(0.1 * n((T, M)) / u, "e2m1")
    return {
        "qc": (q).astype(np.float32),
        "kc": (n((K, T)) / np.sqrt(K) / s).astype(np.float32),
        "qd": (q * 0.995 ** (np.arange(T) + 1.0)).astype(np.float32),
        "st": (n((K, M)) / np.sqrt(K) / s).astype(np.float32),
        "vc_words": p_vc[0],
        "vc_scales": p_vc[1],
        "dm": (np.tril(0.995 ** (np.arange(T)[:, None] - np.arange(T)[None])).T * u).astype(np.float32),
        "g": (n((1024, 1536))).astype(np.float32),
    }


def reference(qc, kc, qd, st, vc_words, vc_scales, dm, g):
    qc_ = mxq(f64(qc), 0, "e4m3")
    kc_ = mxq(f64(kc), 0, "e4m3")
    qd_ = mxq(f64(qd), 0, "e4m3")
    st_ = mxq(f64(st), 0, "e4m3")
    vc_ = unpack_weight(vc_words, vc_scales, "e2m1")
    h_ = mxq((kc_.T @ qc_) * f64(dm), 0, "e4m3")
    y = h_.T @ vc_ + qd_.T @ st_
    return f64(g) * y

@@ -1,0 +1,217 @@
+from contextlib import ExitStack
+
+import concourse.mybir as mybir
+
+K, M, T = 1024, 1536, 1024
+
+F32 = mybir.dt.float32
+BF16 = mybir.dt.bfloat16
+I32 = mybir.dt.int32
+U32 = mybir.dt.uint32
+U8 = mybir.dt.uint8
+FP8X4 = mybir.dt.float8_e4m3fn_x4
+FP4X4 = mybir.dt.float4_e2m1fn_x4
+MULT = mybir.AluOpType.mult
+
+P = 128
+PACK = 4
+PASS = P * PACK
+BANK = 512
+PASSES = 2
+BANKS = 8
+CHUNKS = M // BANK
+
+FLOPS = 2 * K * T * T + 2 * T * T * M + 2 * T * K * M
+BYTES = 4 * (3 * K * T + K * M + T * T // 2 + 2 * T * M) + T * M // 2 + T * M // 32
+
+
+def tile_mix_linattn_tm_mul_kernel(tc, qc, kc, qd, st, vc_words, vc_scales, dm, g, out):
+    nc = tc.nc
+
+    with ExitStack() as ctx:
+        keep = ctx.enter_context(tc.tile_pool(name="keep", bufs=1))
+        raw_t = ctx.enter_context(tc.tile_pool(name="raw_t", bufs=5))
+        raw_m = ctx.enter_context(tc.tile_pool(name="raw_m", bufs=2))
+        stage = ctx.enter_context(tc.tile_pool(name="stage", bufs=4))
+        hstage = ctx.enter_context(tc.tile_pool(name="hstage", bufs=2))
+        psum = ctx.enter_context(tc.psum_pool(name="psum", bufs=BANKS))
+        ctx.enter_context(tc.manual_schedule())
+
+        def planes(name, width):
+            codes = keep.tile([P, width], U32, name=name + "_codes", align_bytes=64)
+            scales = keep.tile([P, width], U8, name=name + "_scales", align_bytes=64)
+            return codes, scales
+
+        kc_mx = [planes("kc%d" % e, T) for e in range(PASSES)]
+        qc_mx = [planes("qc%d" % e, T) for e in range(PASSES)]
+        qd_mx = [planes("qd%d" % e, T) for e in range(PASSES)]
+        st_mx = [planes("st%d" % e, M) for e in range(PASSES)]
+        h_mx = [planes("h0", T), planes("h1", T - PASS)]
+        vc_codes = keep.tile([P, PASSES, 2 * M], U8, align_bytes=64)
+        vc_plane = keep.tile([P, PASSES, M], U8, align_bytes=64)
+
+        def load_pass(pool, tag, rows):
+            width = rows.shape[1]
+            raw = pool.tile([P, PACK, width], F32, name=tag, tag=tag)
+            nc.sync.dma_start(out=raw[:], in_=rows.rearrange("(p i) w -> p i w", i=PACK))
+            return raw
+
+        def copy_on(engine, out_ap, in_ap):
+            if engine == "scalar":
+                nc.scalar.copy(out=out_ap, in_=in_ap)
+            else:
+                nc.vector.tensor_copy(out=out_ap, in_=in_ap)
+
+        def interleave(engine, rows):
+            width = rows.shape[2]
+            grouped = stage.tile([P, width * PACK], BF16, name="grouped", tag="grouped", align_bytes=64)
+            copy_on(
+                engine,
+                grouped[:].rearrange("p (c x i) -> p c i x", x=4, i=PACK),
+                rows.rearrange("p i (c x) -> p c i x", x=4),
+            )
+            return grouped
+
+        def interleave_by_slot(engine, rows):
+            grouped = stage.tile([P, PASS * PACK], BF16, name="grouped", tag="grouped", align_bytes=64)
+            copy_on(
+                engine,
+                grouped[:].rearrange("p (s m i) -> p m i s", s=PACK, i=PACK),
+                rows.rearrange("p i (m s) -> p m i s", s=PACK),
+            )
+            return grouped
+
+        def quantize(mx, c0, grouped):
+            cols = slice(c0, c0 + grouped.shape[1] // PACK)
+            nc.vector.quantize_mx(out=mx[0][:, cols].bitcast(FP8X4), scales=mx[1][:, cols], in_=grouped[:])
+
+        def prepare(raw, mx, arrange):
+            half = raw.shape[2] // 2
+            on_scalar = arrange("scalar", raw[:, :, :half])
+            on_vector = arrange("vector", raw[:, :, half:])
+            quantize(mx, half, on_vector)
+            quantize(mx, 0, on_scalar)
+
+        def prepare_st(raw, mx):
+            width = BANK // 2
+            for c in range(CHUNKS):
+                c0 = c * BANK
+                on_scalar = interleave("scalar", raw[:, :, c0 : c0 + width])
+                on_vector = interleave("vector", raw[:, :, c0 + width : c0 + BANK])
+                quantize(mx, c0, on_scalar)
+                quantize(mx, c0 + width, on_vector)
+
+        def e4m3(mx, cols):
+            return mx[0][:, cols].bitcast(FP8X4), mx[1][:, cols]
+
+        def mx_pass(acc, stationary, moving, start, stop):
+            nc.tensor.matmul_mx(
+                out=acc[:], lhsT=stationary[0], lhsT_scale=stationary[1],
+                rhs=moving[0], rhs_scale=moving[1], start=start, stop=stop,
+            )
+
+        nc.vector.memset(vc_plane[:].bitcast(I32), 0)
+        for r in range(4):
+            nc.scalar.dma_start(
+                out=vc_plane[r:P:32, :, :].bitcast(I32),
+                in_=vc_scales[:, r:16:4, :].rearrange("a q n -> q a n").bitcast(I32),
+            )
+
+        kc_raw, qc_raw = [], []
+        for e in range(PASSES):
+            kc_raw.append(load_pass(raw_t, "raw_t", kc[e * PASS : (e + 1) * PASS, :]))
+            qc_raw.append(load_pass(raw_t, "raw_t", qc[e * PASS : (e + 1) * PASS, :]))
+        dm_raw = [load_pass(raw_t, "raw_t", dm[:PASS, :])]
+
+        prepare(kc_raw[0], kc_mx[0], interleave_by_slot)
+        dm_raw.append(load_pass(raw_t, "raw_t", dm[PASS:, PASS:]))
+        nc.sync.dma_start(
+            out=vc_codes[:].bitcast(I32), in_=vc_words.rearrange("a p b -> p a b").bitcast(I32)
+        )
+        st_raw = [load_pass(raw_m, "raw_m", st[:PASS, :])]
+        prepare(qc_raw[0], qc_mx[0], interleave)
+        qd_raw = [load_pass(raw_t, "raw_t", qd[:PASS, :])]
+        st_raw.append(load_pass(raw_m, "raw_m", st[PASS:, :]))
+        prepare(kc_raw[1], kc_mx[1], interleave_by_slot)
+        qd_raw.append(load_pass(raw_t, "raw_t", qd[PASS:, :]))
+        prepare(qc_raw[1], qc_mx[1], interleave)
+
+        pending = []
+        for a, t0 in ((0, PASS), (0, 0), (1, PASS)):
+            h_rows = hstage.tile([P, PACK, BANK], BF16, name="h_rows", tag="h_rows")
+            local = slice(t0 - a * PASS, t0 - a * PASS + BANK)
+            for s in range(PACK):
+                acc = psum.tile([P, BANK], F32, name="acc", tag="acc")
+                j_cols = slice(a * PASS + s * P, a * PASS + (s + 1) * P)
+                for e in range(PASSES):
+                    mx_pass(acc, e4m3(kc_mx[e], j_cols), e4m3(qc_mx[e], slice(t0, t0 + BANK)),
+                            e == 0, e == PASSES - 1)
+                nc.vector.tensor_tensor(out=h_rows[:, s, :], in0=acc[:], in1=dm_raw[a][:, s, local], op=MULT)
+            if pending:
+                quantize(*pending.pop())
+            pending.append((h_mx[a], local.start, interleave("scalar", h_rows[:])))
+        quantize(*pending.pop())
+
+        tiles = [4, 5, 6, 7, 0, 1, 2, 3]
+        groups = [(r, c) for r in tiles for c in range(CHUNKS)]
+
+        def value_passes(acc, r, c):
+            for a in range(r * P // PASS + 1):
+                t_cols = slice(r * P - a * PASS, (r + 1) * P - a * PASS)
+                moving = (
+                    vc_codes[:, a, 2 * c * BANK : 2 * (c + 1) * BANK].bitcast(FP4X4),
+                    vc_plane[:, a, c * BANK : (c + 1) * BANK],
+                )
+                mx_pass(acc, e4m3(h_mx[a], t_cols), moving, a == 0, False)
+
+        def state_pass(acc, r, c, e):
+            mx_pass(acc, e4m3(qd_mx[e], slice(r * P, (r + 1) * P)),
+                    e4m3(st_mx[e], slice(c * BANK, (c + 1) * BANK)), False, e == PASSES - 1)
+
+        early = []
+        for r, c in groups[:BANKS]:
+            acc = psum.tile([P, BANK], F32, name="acc", tag="acc")
+            value_passes(acc, r, c)
+            early.append(acc)
+
+        prepare_st(st_raw[0], st_mx[0])
+        g_half = {}
+
+        def load_gate(half):
+            g_half[half] = raw_m.tile([P, PACK, M], F32, name="raw_m", tag="raw_m")
+            for x in range(PACK):
+                r = half * PACK + x
+                nc.sync.dma_start(out=g_half[half][:, x, :], in_=g[r * P : (r + 1) * P, :])
+
+        load_gate(1)
+        prepare(qd_raw[0], qd_mx[0], interleave)
+        for acc, (r, c) in zip(early, groups):
+            state_pass(acc, r, c, 0)
+        prepare_st(st_raw[1], st_mx[1])
+        load_gate(0)
+
+        def prepare_last(engine, r):
+            return qd_mx[1], r * P, interleave(engine, qd_raw[1][:, :, r * P : (r + 1) * P])
+
+        lead = 3
+        ready = [prepare_last("vector" if n == 0 else "scalar", r) for n, r in enumerate(tiles[:lead])]
+        for item in ready:
+            quantize(*item)
+        for acc, (r, c) in zip(early, groups):
+            state_pass(acc, r, c, 1)
+
+        accs = list(early)
+        for n, (r, c) in enumerate(groups):
+            if c == 0 and n // CHUNKS + lead < len(tiles):
+                quantize(*prepare_last("scalar", tiles[n // CHUNKS + lead]))
+            gate = g_half[r // PACK][:, r % PACK, c * BANK : (c + 1) * BANK]
+            nc.vector.tensor_tensor(out=gate, in0=accs[n][:], in1=gate, op=MULT)
+            if n + BANKS < len(groups):
+                r2, c2 = groups[n + BANKS]
+                acc = psum.tile([P, BANK], F32, name="acc", tag="acc")
+                value_passes(acc, r2, c2)
+                for e in range(PASSES):
+                    state_pass(acc, r2, c2, e)
+                accs.append(acc)
+            if c == CHUNKS - 1:
+                nc.sync.dma_start(out=out[r * P : (r + 1) * P, :], in_=g_half[r // PACK][:, r % PACK, :])

@@ -130,8 +130,8 @@ def tile_mix_linattn_tm_mul_kernel(tc, qc, kc, qd, st, vc_words, vc_scales, dm, 
         )
         st_raw = [load_pass(raw_m, "raw_m", st[:PASS, :])]
         prepare(qc_raw[0], qc_mx[0], interleave)
-        qd_raw = [load_pass(raw_t, "raw_t", qd[:PASS, :])]
         st_raw.append(load_pass(raw_m, "raw_m", st[PASS:, :]))
+        qd_raw = [load_pass(raw_t, "raw_t", qd[:PASS, :])]
         prepare(kc_raw[1], kc_mx[1], interleave_by_slot)
         qd_raw.append(load_pass(raw_t, "raw_t", qd[PASS:, :]))
         prepare(qc_raw[1], qc_mx[1], interleave)
@@ -149,7 +149,7 @@ def tile_mix_linattn_tm_mul_kernel(tc, qc, kc, qd, st, vc_words, vc_scales, dm, 
                 nc.vector.tensor_tensor(out=h_rows[:, s, :], in0=acc[:], in1=dm_raw[a][:, s, local], op=MULT)
             if pending:
                 quantize(*pending.pop())
-            pending.append((h_mx[a], local.start, interleave("scalar", h_rows[:])))
+            pending.append((h_mx[a], local.start, interleave_by_slot("scalar", h_rows[:])))
         quantize(*pending.pop())
 
         tiles = [4, 5, 6, 7, 0, 1, 2, 3]
@@ -179,31 +179,22 @@ def tile_mix_linattn_tm_mul_kernel(tc, qc, kc, qd, st, vc_words, vc_scales, dm, 
 
         def load_gate(half):
             g_half[half] = raw_m.tile([P, PACK, M], F32, name="raw_m", tag="raw_m")
-            for x in range(PACK):
-                r = half * PACK + x
-                nc.sync.dma_start(out=g_half[half][:, x, :], in_=g[r * P : (r + 1) * P, :])
+            rows = g[half * PASS : (half + 1) * PASS, :].rearrange("(p u) n -> p u n", u=PACK)
+            for u in range(0, PACK, 2):
+                nc.sync.dma_start(out=g_half[half][:, u : u + 2, :], in_=rows[:, u : u + 2, :])
 
         load_gate(1)
-        prepare(qd_raw[0], qd_mx[0], interleave)
-        for acc, (r, c) in zip(early, groups):
-            state_pass(acc, r, c, 0)
         prepare_st(st_raw[1], st_mx[1])
         load_gate(0)
+        for e in range(PASSES):
+            prepare(qd_raw[e], qd_mx[e], interleave_by_slot)
+            for acc, (r, c) in zip(early, groups):
+                state_pass(acc, r, c, e)
 
-        def prepare_last(engine, r):
-            return qd_mx[1], r * P, interleave(engine, qd_raw[1][:, :, r * P : (r + 1) * P])
-
-        lead = 3
-        ready = [prepare_last("vector" if n == 0 else "scalar", r) for n, r in enumerate(tiles[:lead])]
-        for item in ready:
-            quantize(*item)
-        for acc, (r, c) in zip(early, groups):
-            state_pass(acc, r, c, 1)
+        stores = {7: 4, 1: 0, 2: 2, 3: 3}
 
         accs = list(early)
         for n, (r, c) in enumerate(groups):
-            if c == 0 and n // CHUNKS + lead < len(tiles):
-                quantize(*prepare_last("scalar", tiles[n // CHUNKS + lead]))
             gate = g_half[r // PACK][:, r % PACK, c * BANK : (c + 1) * BANK]
             nc.vector.tensor_tensor(out=gate, in0=accs[n][:], in1=gate, op=MULT)
             if n + BANKS < len(groups):
@@ -213,5 +204,8 @@ def tile_mix_linattn_tm_mul_kernel(tc, qc, kc, qd, st, vc_words, vc_scales, dm, 
                 for e in range(PASSES):
                     state_pass(acc, r2, c2, e)
                 accs.append(acc)
-            if c == CHUNKS - 1:
-                nc.sync.dma_start(out=out[r * P : (r + 1) * P, :], in_=g_half[r // PACK][:, r % PACK, :])
+            if c == CHUNKS - 1 and r in stores:
+                half = r // PACK
+                slots = slice(stores[r] % PACK, r % PACK + 1)
+                rows = out[half * PASS : (half + 1) * PASS, :].rearrange("(p u) n -> p u n", u=PACK)
+                nc.sync.dma_start(out=rows[:, slots, :], in_=g_half[half][:, slots, :])

from contextlib import ExitStack

import concourse.mybir as mybir

K, M, T = 1024, 1536, 1024

F32 = mybir.dt.float32
BF16 = mybir.dt.bfloat16
I32 = mybir.dt.int32
U32 = mybir.dt.uint32
U8 = mybir.dt.uint8
FP8X4 = mybir.dt.float8_e4m3fn_x4
FP4X4 = mybir.dt.float4_e2m1fn_x4
MULT = mybir.AluOpType.mult

P = 128
PACK = 4
PASS = P * PACK
BANK = 512
PASSES = 2
BANKS = 8
CHUNKS = M // BANK

FLOPS = 2 * K * T * T + 2 * T * T * M + 2 * T * K * M
BYTES = 4 * (3 * K * T + K * M + T * T // 2 + 2 * T * M) + T * M // 2 + T * M // 32


def tile_mix_linattn_tm_mul_kernel(tc, qc, kc, qd, st, vc_words, vc_scales, dm, g, out):
    nc = tc.nc

    with ExitStack() as ctx:
        keep = ctx.enter_context(tc.tile_pool(name="keep", bufs=1))
        raw_t = ctx.enter_context(tc.tile_pool(name="raw_t", bufs=5))
        raw_m = ctx.enter_context(tc.tile_pool(name="raw_m", bufs=2))
        stage = ctx.enter_context(tc.tile_pool(name="stage", bufs=4))
        hstage = ctx.enter_context(tc.tile_pool(name="hstage", bufs=2))
        psum = ctx.enter_context(tc.psum_pool(name="psum", bufs=BANKS))
        ctx.enter_context(tc.manual_schedule())

        def planes(name, width):
            codes = keep.tile([P, width], U32, name=name + "_codes", align_bytes=64)
            scales = keep.tile([P, width], U8, name=name + "_scales", align_bytes=64)
            return codes, scales

        kc_mx = [planes("kc%d" % e, T) for e in range(PASSES)]
        qc_mx = [planes("qc%d" % e, T) for e in range(PASSES)]
        qd_mx = [planes("qd%d" % e, T) for e in range(PASSES)]
        st_mx = [planes("st%d" % e, M) for e in range(PASSES)]
        h_mx = [planes("h0", T), planes("h1", T - PASS)]
        vc_codes = keep.tile([P, PASSES, 2 * M], U8, align_bytes=64)
        vc_plane = keep.tile([P, PASSES, M], U8, align_bytes=64)

        def load_pass(pool, tag, rows):
            width = rows.shape[1]
            raw = pool.tile([P, PACK, width], F32, name=tag, tag=tag)
            nc.sync.dma_start(out=raw[:], in_=rows.rearrange("(p i) w -> p i w", i=PACK))
            return raw

        def copy_on(engine, out_ap, in_ap):
            if engine == "scalar":
                nc.scalar.copy(out=out_ap, in_=in_ap)
            else:
                nc.vector.tensor_copy(out=out_ap, in_=in_ap)

        def interleave(engine, rows):
            width = rows.shape[2]
            grouped = stage.tile([P, width * PACK], BF16, name="grouped", tag="grouped", align_bytes=64)
            copy_on(
                engine,
                grouped[:].rearrange("p (c x i) -> p c i x", x=4, i=PACK),
                rows.rearrange("p i (c x) -> p c i x", x=4),
            )
            return grouped

        def interleave_by_slot(engine, rows):
            grouped = stage.tile([P, PASS * PACK], BF16, name="grouped", tag="grouped", align_bytes=64)
            copy_on(
                engine,
                grouped[:].rearrange("p (s m i) -> p m i s", s=PACK, i=PACK),
                rows.rearrange("p i (m s) -> p m i s", s=PACK),
            )
            return grouped

        def quantize(mx, c0, grouped):
            cols = slice(c0, c0 + grouped.shape[1] // PACK)
            nc.vector.quantize_mx(out=mx[0][:, cols].bitcast(FP8X4), scales=mx[1][:, cols], in_=grouped[:])

        def prepare(raw, mx, arrange):
            half = raw.shape[2] // 2
            on_scalar = arrange("scalar", raw[:, :, :half])
            on_vector = arrange("vector", raw[:, :, half:])
            quantize(mx, half, on_vector)
            quantize(mx, 0, on_scalar)

        def prepare_st(raw, mx):
            width = BANK // 2
            for c in range(CHUNKS):
                c0 = c * BANK
                on_scalar = interleave("scalar", raw[:, :, c0 : c0 + width])
                on_vector = interleave("vector", raw[:, :, c0 + width : c0 + BANK])
                quantize(mx, c0, on_scalar)
                quantize(mx, c0 + width, on_vector)

        def e4m3(mx, cols):
            return mx[0][:, cols].bitcast(FP8X4), mx[1][:, cols]

        def mx_pass(acc, stationary, moving, start, stop):
            nc.tensor.matmul_mx(
                out=acc[:], lhsT=stationary[0], lhsT_scale=stationary[1],
                rhs=moving[0], rhs_scale=moving[1], start=start, stop=stop,
            )

        nc.vector.memset(vc_plane[:].bitcast(I32), 0)
        for r in range(4):
            nc.scalar.dma_start(
                out=vc_plane[r:P:32, :, :].bitcast(I32),
                in_=vc_scales[:, r:16:4, :].rearrange("a q n -> q a n").bitcast(I32),
            )

        kc_raw, qc_raw = [], []
        for e in range(PASSES):
            kc_raw.append(load_pass(raw_t, "raw_t", kc[e * PASS : (e + 1) * PASS, :]))
            qc_raw.append(load_pass(raw_t, "raw_t", qc[e * PASS : (e + 1) * PASS, :]))
        dm_raw = [load_pass(raw_t, "raw_t", dm[:PASS, :])]

        prepare(kc_raw[0], kc_mx[0], interleave_by_slot)
        dm_raw.append(load_pass(raw_t, "raw_t", dm[PASS:, PASS:]))
        nc.sync.dma_start(
            out=vc_codes[:].bitcast(I32), in_=vc_words.rearrange("a p b -> p a b").bitcast(I32)
        )
        st_raw = [load_pass(raw_m, "raw_m", st[:PASS, :])]
        prepare(qc_raw[0], qc_mx[0], interleave)
        st_raw.append(load_pass(raw_m, "raw_m", st[PASS:, :]))
        qd_raw = [load_pass(raw_t, "raw_t", qd[:PASS, :])]
        prepare(kc_raw[1], kc_mx[1], interleave_by_slot)
        qd_raw.append(load_pass(raw_t, "raw_t", qd[PASS:, :]))
        prepare(qc_raw[1], qc_mx[1], interleave)

        pending = []
        for a, t0 in ((0, PASS), (0, 0), (1, PASS)):
            h_rows = hstage.tile([P, PACK, BANK], BF16, name="h_rows", tag="h_rows")
            local = slice(t0 - a * PASS, t0 - a * PASS + BANK)
            for s in range(PACK):
                acc = psum.tile([P, BANK], F32, name="acc", tag="acc")
                j_cols = slice(a * PASS + s * P, a * PASS + (s + 1) * P)
                for e in range(PASSES):
                    mx_pass(acc, e4m3(kc_mx[e], j_cols), e4m3(qc_mx[e], slice(t0, t0 + BANK)),
                            e == 0, e == PASSES - 1)
                nc.vector.tensor_tensor(out=h_rows[:, s, :], in0=acc[:], in1=dm_raw[a][:, s, local], op=MULT)
            if pending:
                quantize(*pending.pop())
            pending.append((h_mx[a], local.start, interleave_by_slot("scalar", h_rows[:])))
        quantize(*pending.pop())

        tiles = [4, 5, 6, 7, 0, 1, 2, 3]
        groups = [(r, c) for r in tiles for c in range(CHUNKS)]

        def value_passes(acc, r, c):
            for a in range(r * P // PASS + 1):
                t_cols = slice(r * P - a * PASS, (r + 1) * P - a * PASS)
                moving = (
                    vc_codes[:, a, 2 * c * BANK : 2 * (c + 1) * BANK].bitcast(FP4X4),
                    vc_plane[:, a, c * BANK : (c + 1) * BANK],
                )
                mx_pass(acc, e4m3(h_mx[a], t_cols), moving, a == 0, False)

        def state_pass(acc, r, c, e):
            mx_pass(acc, e4m3(qd_mx[e], slice(r * P, (r + 1) * P)),
                    e4m3(st_mx[e], slice(c * BANK, (c + 1) * BANK)), False, e == PASSES - 1)

        early = []
        for r, c in groups[:BANKS]:
            acc = psum.tile([P, BANK], F32, name="acc", tag="acc")
            value_passes(acc, r, c)
            early.append(acc)

        prepare_st(st_raw[0], st_mx[0])
        g_half = {}

        def load_gate(half):
            g_half[half] = raw_m.tile([P, PACK, M], F32, name="raw_m", tag="raw_m")
            rows = g[half * PASS : (half + 1) * PASS, :].rearrange("(p u) n -> p u n", u=PACK)
            for u in range(0, PACK, 2):
                nc.sync.dma_start(out=g_half[half][:, u : u + 2, :], in_=rows[:, u : u + 2, :])

        load_gate(1)
        prepare_st(st_raw[1], st_mx[1])
        load_gate(0)
        for e in range(PASSES):
            prepare(qd_raw[e], qd_mx[e], interleave_by_slot)
            for acc, (r, c) in zip(early, groups):
                state_pass(acc, r, c, e)

        stores = {7: 4, 1: 0, 2: 2, 3: 3}

        accs = list(early)
        for n, (r, c) in enumerate(groups):
            gate = g_half[r // PACK][:, r % PACK, c * BANK : (c + 1) * BANK]
            nc.vector.tensor_tensor(out=gate, in0=accs[n][:], in1=gate, op=MULT)
            if n + BANKS < len(groups):
                r2, c2 = groups[n + BANKS]
                acc = psum.tile([P, BANK], F32, name="acc", tag="acc")
                value_passes(acc, r2, c2)
                for e in range(PASSES):
                    state_pass(acc, r2, c2, e)
                accs.append(acc)
            if c == CHUNKS - 1 and r in stores:
                half = r // PACK
                slots = slice(stores[r] % PACK, r % PACK + 1)
                rows = out[half * PASS : (half + 1) * PASS, :].rearrange("(p u) n -> p u n", u=PACK)
                nc.sync.dma_start(out=rows[:, slots, :], in_=g_half[half][:, slots, :])
